import numpy as np
import ml_dtypes


def mxq(x, axis, fmt="e4m3"):
    dtype, down = {"e4m3": (ml_dtypes.float8_e4m3fn, 7), "e5m2": (ml_dtypes.float8_e5m2, 14)}[fmt]
    v = np.moveaxis(np.asarray(x, np.float32).astype(ml_dtypes.bfloat16).astype(np.float64), axis, -1)
    blocks = v.reshape(v.shape[:-1] + (-1, 32))
    amax = np.abs(blocks).max(-1, keepdims=True)
    byte = np.maximum(np.where(amax > 0, np.frexp(amax)[1] - 1 + 127, 0) - down, 1)
    scale = np.exp2(byte - 127.0)
    codes = (blocks / scale).astype(np.float32).astype(dtype).astype(np.float64)
    return np.moveaxis((codes * scale).reshape(v.shape), -1, axis)


WIDE = False


def mx_kscale(k, group=512):
    if not WIDE:
        return np.ones(k)
    levels = np.array([18, -18])
    if group != 512:
        return np.exp2(np.random.permutation(np.resize(levels, k // group))).repeat(group)
    if k % 512:
        return np.exp2(np.random.permutation(np.resize(levels, k // 32))).repeat(32)
    a = np.empty((k // 512, 16))
    for p in range(k // 512):
        a[p, :8] = np.random.permutation(np.resize(levels, 8))
        for g in range(8):
            far = levels[np.abs(levels - a[p, g]) >= 10]
            a[p, g + 8] = far[np.random.randint(len(far))]
    return np.exp2(a.ravel()).repeat(32)


def f64(x):
    return np.asarray(x).astype(np.float64)


H, D, N = 8, 128, 512


def setup_inputs():
    n = np.random.standard_normal
    s = mx_kscale(D, 0)[:, None]
    S = n((H, D, 128)) / np.sqrt(D)
    return {
        "q": n((H, D, N)).astype(np.float32),
        "qa": (np.random.uniform(0.5, 2.0, (D, 1)) * s).astype(np.float32),
        "S": (S / s).astype(np.float32),
        "og": n((H, N, 128)).astype(np.float32),
    }


def reference(q, qa, S, og):
    fq = (np.where(f64(q) > 0, f64(q) + 1.0, np.exp(np.minimum(f64(q), 0.0)))) * f64(qa)
    y = mxq(fq, 1, "e4m3").transpose(0, 2, 1) @ mxq(f64(S), 1, "e4m3")
    y = y / (1.0 + np.exp(-f64(og)))
    return y

@@ -1,0 +1,160 @@
+from contextlib import ExitStack
+
+import concourse.mybir as mybir
+
+H, D, N, E = 8, 128, 512, 128
+FLOPS = 2 * H * N * D * E
+
+F32 = mybir.dt.float32
+BF16 = mybir.dt.bfloat16
+U32 = mybir.dt.uint32
+U8 = mybir.dt.uint8
+FP8X4 = mybir.dt.float8_e4m3fn_x4
+ACT = mybir.ActivationFunctionType
+ALU = mybir.AluOpType
+
+P = 128
+PACK = 4
+ROWS = D // PACK
+HEADS_PER_SET = P // ROWS
+SETS = H // HEADS_PER_SET
+DEAL = N // P
+
+
+def tile_rows_read_elu1_gate_kernel(tc, q, qa, S, og, out):
+    nc = tc.nc
+    with ExitStack() as ctx:
+        sb = ctx.enter_context(tc.tile_pool(name="sb", bufs=1))
+        ps = ctx.enter_context(tc.psum_pool(name="ps", bufs=1))
+        ctx.enter_context(tc.manual_schedule())
+
+        def tiles(pool, name, count, shape, dtype):
+            return [pool.tile(shape, dtype, name="%s%d" % (name, i), align_bytes=64) for i in range(count)]
+
+        q_raw = [tiles(sb, "q_raw%d_" % s, PACK, [P, N], F32) for s in range(SETS)]
+        q_neg = [tiles(sb, "q_neg%d_" % s, PACK, [P, N], F32) for s in range(SETS)]
+        q_exp = [tiles(sb, "q_exp%d_" % s, PACK, [P, N], F32) for s in range(SETS)]
+        phi = tiles(sb, "phi", SETS, [P, PACK, N], F32)
+        q_bf = tiles(sb, "q_bf", SETS, [P, DEAL, P, PACK], BF16)
+        q_codes = tiles(sb, "q_codes", SETS, [P, N], U32)
+        q_scales = tiles(sb, "q_scales", SETS, [P, N], U8)
+        s_raw = tiles(sb, "s_raw", SETS, [P, PACK, E], F32)
+        s_bf = tiles(sb, "s_bf", SETS, [P, E, PACK], BF16)
+        s_codes = tiles(sb, "s_codes", SETS, [P, E], U32)
+        s_scales = tiles(sb, "s_scales", SETS, [P, E], U8)
+        og_raw = tiles(sb, "og_raw", H, [P, DEAL * E], F32)
+        og_tanh = tiles(sb, "og_tanh", H, [P, DEAL * E], F32)
+        result = tiles(sb, "result", H, [P, DEAL * E], F32)
+        qa4 = sb.tile([P, PACK], F32, align_bytes=64)
+        y = [ps.tile([P, DEAL * E], F32, name="y%d" % h) for h in range(H)]
+
+        def heads(s):
+            return slice(s * HEADS_PER_SET, (s + 1) * HEADS_PER_SET)
+
+        def load_q(s):
+            rows = q[heads(s)].rearrange("c (p j) n -> (c p) j n", j=PACK)
+            for j in range(PACK):
+                nc.sync.dma_start(out=q_raw[s][j][:], in_=rows[:, j, :])
+
+        def load_state(s):
+            nc.sync.dma_start(out=s_raw[s][:], in_=S[heads(s)].rearrange("c (p j) e -> (c p) j e", j=PACK))
+
+        def load_gate(h):
+            nc.sync.dma_start(out=og_raw[h][:], in_=og[h].rearrange("(m r) e -> m (r e)", r=DEAL))
+
+        def clamp_vector(s, j):
+            nc.vector.tensor_scalar(out=q_neg[s][j][:], in0=q_raw[s][j][:], scalar1=0.0, scalar2=-1.0,
+                                    op0=ALU.min, op1=ALU.mult)
+
+        def clamp_scalar(s, j):
+            nc.scalar.activation(out=q_neg[s][j][:], in_=q_raw[s][j][:], func=ACT.Relu, scale=-1.0)
+
+        def exp(s, j):
+            nc.scalar.activation(out=q_exp[s][j][:], in_=q_neg[s][j][:], func=ACT.Exp, scale=-1.0)
+
+        def combine(s, j):
+            nc.vector.scalar_tensor_tensor(out=phi[s][:, j, :], in0=q_raw[s][j][:], scalar=0.0,
+                                           in1=q_exp[s][j][:], op0=ALU.max, op1=ALU.add)
+
+        def weigh(s):
+            nc.vector.tensor_tensor(
+                out=q_bf[s][:].rearrange("p r m j -> p m j r"),
+                in0=phi[s][:].rearrange("p j (m r) -> p m j r", r=DEAL),
+                in1=qa4[:].unsqueeze(1).unsqueeze(3).to_broadcast([P, P, PACK, DEAL]),
+                op=ALU.mult)
+
+        def quantize_q(s):
+            nc.vector.quantize_mx(out=q_codes[s][:].bitcast(FP8X4), scales=q_scales[s][:],
+                                  in_=q_bf[s][:].rearrange("p r m j -> p (r m j)"))
+
+        def round_state(s):
+            nc.scalar.activation(
+                out=s_bf[s][:].rearrange("p (c i) j -> p c j i", i=4),
+                in_=s_raw[s][:].rearrange("p j (c i) -> p c j i", i=4),
+                func=ACT.Copy, scale=0.5)
+
+        def quantize_state(s):
+            nc.vector.quantize_mx(out=s_codes[s][:].bitcast(FP8X4), scales=s_scales[s][:],
+                                  in_=s_bf[s][:].rearrange("p e j -> p (e j)"))
+
+        def multiply(s):
+            for r in range(DEAL):
+                cols = slice(r * P, (r + 1) * P)
+                for c in range(HEADS_PER_SET):
+                    rows = slice(c * ROWS, (c + 1) * ROWS)
+                    nc.tensor.matmul_mx(
+                        out=y[s * HEADS_PER_SET + c][:, r * E:(r + 1) * E],
+                        lhsT=q_codes[s][rows, cols].bitcast(FP8X4), lhsT_scale=q_scales[s][rows, cols],
+                        rhs=s_codes[s][rows, :].bitcast(FP8X4), rhs_scale=s_scales[s][rows, :],
+                        start=True, stop=True)
+
+        def tanh(h):
+            nc.scalar.activation(out=og_tanh[h][:], in_=og_raw[h][:], func=ACT.Tanh, scale=0.5)
+
+        def gate(h):
+            nc.vector.scalar_tensor_tensor(out=result[h][:], in0=og_tanh[h][:], scalar=1.0, in1=y[h][:],
+                                           op0=ALU.add, op1=ALU.mult)
+            nc.sync.dma_start(out=out[h].rearrange("(m r) e -> m (r e)", r=DEAL), in_=result[h][:])
+
+        load_q(0)
+        load_state(0)
+        nc.sync.dma_start(
+            out=qa4[:],
+            in_=qa.rearrange("d o -> (d o)").partition_broadcast(HEADS_PER_SET).rearrange("c (p j) -> c p j", j=PACK))
+        load_q(1)
+        load_state(1)
+        for h in range(H):
+            load_gate(h)
+
+        clamp_vector(0, 0)
+        exp(0, 0)
+        for j in range(1, PACK):
+            clamp_vector(0, j)
+            exp(0, j)
+            combine(0, j - 1)
+        combine(0, PACK - 1)
+        clamp_vector(1, 0)
+        round_state(0)
+        exp(1, 0)
+        for j in range(1, PACK):
+            clamp_scalar(1, j)
+            exp(1, j)
+        tanh(0)
+        round_state(1)
+        for h in range(1, H):
+            tanh(h)
+        weigh(0)
+        combine(1, 0)
+        quantize_state(0)
+        quantize_q(0)
+        multiply(0)
+        for j in range(1, PACK):
+            combine(1, j)
+        gate(0)
+        weigh(1)
+        gate(1)
+        quantize_state(1)
+        quantize_q(1)
+        multiply(1)
+        for h in range(2, H):
+            gate(h)

@@ -34,10 +34,11 @@ def tile_rows_read_elu1_gate_kernel(tc, q, qa, S, og, out):
         q_raw = [tiles(sb, "q_raw%d_" % s, PACK, [P, N], F32) for s in range(SETS)]
         q_neg = [tiles(sb, "q_neg%d_" % s, PACK, [P, N], F32) for s in range(SETS)]
         q_exp = [tiles(sb, "q_exp%d_" % s, PACK, [P, N], F32) for s in range(SETS)]
-        phi = tiles(sb, "phi", SETS, [P, PACK, N], F32)
-        q_bf = tiles(sb, "q_bf", SETS, [P, DEAL, P, PACK], BF16)
-        q_codes = tiles(sb, "q_codes", SETS, [P, N], U32)
-        q_scales = tiles(sb, "q_scales", SETS, [P, N], U8)
+        pos = tiles(sb, "pos", SETS, [P, PACK, N], F32)
+        neg = tiles(sb, "neg", SETS, [P, PACK, N], F32)
+        q_bf = [tiles(sb, "q_bf%d_" % s, 2, [P, 2, P, PACK], BF16) for s in range(SETS)]
+        q_codes = [tiles(sb, "q_codes%d_" % s, 2, [P, 2 * P], U32) for s in range(SETS)]
+        q_scales = [tiles(sb, "q_scales%d_" % s, 2, [P, 2 * P], U8) for s in range(SETS)]
         s_raw = tiles(sb, "s_raw", SETS, [P, PACK, E], F32)
         s_bf = tiles(sb, "s_bf", SETS, [P, E, PACK], BF16)
         s_codes = tiles(sb, "s_codes", SETS, [P, E], U32)
@@ -51,10 +52,9 @@ def tile_rows_read_elu1_gate_kernel(tc, q, qa, S, og, out):
         def heads(s):
             return slice(s * HEADS_PER_SET, (s + 1) * HEADS_PER_SET)
 
-        def load_q(s):
+        def load_q(s, j):
             rows = q[heads(s)].rearrange("c (p j) n -> (c p) j n", j=PACK)
-            for j in range(PACK):
-                nc.sync.dma_start(out=q_raw[s][j][:], in_=rows[:, j, :])
+            nc.sync.dma_start(out=q_raw[s][j][:], in_=rows[:, j, :])
 
         def load_state(s):
             nc.sync.dma_start(out=s_raw[s][:], in_=S[heads(s)].rearrange("c (p j) e -> (c p) j e", j=PACK))
@@ -72,20 +72,27 @@ def tile_rows_read_elu1_gate_kernel(tc, q, qa, S, og, out):
         def exp(s, j):
             nc.scalar.activation(out=q_exp[s][j][:], in_=q_neg[s][j][:], func=ACT.Exp, scale=-1.0)
 
-        def combine(s, j):
-            nc.vector.scalar_tensor_tensor(out=phi[s][:, j, :], in0=q_raw[s][j][:], scalar=0.0,
-                                           in1=q_exp[s][j][:], op0=ALU.max, op1=ALU.add)
+        def pos_vector(s, j):
+            nc.vector.tensor_scalar(out=pos[s][:, j, :], in0=q_raw[s][j][:], scalar1=0.0, scalar2=qa4[:, j:j + 1],
+                                    op0=ALU.max, op1=ALU.mult)
 
-        def weigh(s):
+        def neg_scalar(s, j):
+            nc.scalar.activation(out=neg[s][:, j, :], in_=q_exp[s][j][:], func=ACT.Copy, scale=qa4[:, j:j + 1])
+
+        def neg_vector(s, j):
+            nc.vector.tensor_scalar(out=neg[s][:, j, :], in0=q_exp[s][j][:], scalar1=qa4[:, j:j + 1], scalar2=None,
+                                    op0=ALU.mult)
+
+        def combine(s, a):
             nc.vector.tensor_tensor(
-                out=q_bf[s][:].rearrange("p r m j -> p m j r"),
-                in0=phi[s][:].rearrange("p j (m r) -> p m j r", r=DEAL),
-                in1=qa4[:].unsqueeze(1).unsqueeze(3).to_broadcast([P, P, PACK, DEAL]),
-                op=ALU.mult)
+                out=q_bf[s][a][:].rearrange("p b m j -> p m j b"),
+                in0=pos[s][:].rearrange("p j (m a b) -> p a m j b", a=2, b=2)[:, a],
+                in1=neg[s][:].rearrange("p j (m a b) -> p a m j b", a=2, b=2)[:, a],
+                op=ALU.add)
 
-        def quantize_q(s):
-            nc.vector.quantize_mx(out=q_codes[s][:].bitcast(FP8X4), scales=q_scales[s][:],
-                                  in_=q_bf[s][:].rearrange("p r m j -> p (r m j)"))
+        def quantize_q(s, a):
+            nc.vector.quantize_mx(out=q_codes[s][a][:].bitcast(FP8X4), scales=q_scales[s][a][:],
+                                  in_=q_bf[s][a][:].rearrange("p b m j -> p (b m j)"))
 
         def round_state(s):
             nc.scalar.activation(
@@ -97,14 +104,15 @@ def tile_rows_read_elu1_gate_kernel(tc, q, qa, S, og, out):
             nc.vector.quantize_mx(out=s_codes[s][:].bitcast(FP8X4), scales=s_scales[s][:],
                                   in_=s_bf[s][:].rearrange("p e j -> p (e j)"))
 
-        def multiply(s):
-            for r in range(DEAL):
-                cols = slice(r * P, (r + 1) * P)
-                for c in range(HEADS_PER_SET):
-                    rows = slice(c * ROWS, (c + 1) * ROWS)
+        def multiply(s, a):
+            for c in range(HEADS_PER_SET):
+                rows = slice(c * ROWS, (c + 1) * ROWS)
+                for b in range(2):
+                    cols = slice(b * P, (b + 1) * P)
+                    r = 2 * a + b
                     nc.tensor.matmul_mx(
                         out=y[s * HEADS_PER_SET + c][:, r * E:(r + 1) * E],
-                        lhsT=q_codes[s][rows, cols].bitcast(FP8X4), lhsT_scale=q_scales[s][rows, cols],
+                        lhsT=q_codes[s][a][rows, cols].bitcast(FP8X4), lhsT_scale=q_scales[s][a][rows, cols],
                         rhs=s_codes[s][rows, :].bitcast(FP8X4), rhs_scale=s_scales[s][rows, :],
                         start=True, stop=True)
 
@@ -116,45 +124,59 @@ def tile_rows_read_elu1_gate_kernel(tc, q, qa, S, og, out):
                                            op0=ALU.add, op1=ALU.mult)
             nc.sync.dma_start(out=out[h].rearrange("(m r) e -> m (r e)", r=DEAL), in_=result[h][:])
 
-        load_q(0)
-        load_state(0)
-        nc.sync.dma_start(
+        nc.scalar.dma_start(
             out=qa4[:],
             in_=qa.rearrange("d o -> (d o)").partition_broadcast(HEADS_PER_SET).rearrange("c (p j) -> c p j", j=PACK))
-        load_q(1)
+        for j in range(PACK):
+            load_q(0, j)
+        load_q(1, 0)
+        load_state(0)
+        for j in range(1, PACK):
+            load_q(1, j)
+        load_gate(0)
         load_state(1)
-        for h in range(H):
+        for h in range(1, H):
             load_gate(h)
 
-        clamp_vector(0, 0)
+        clamp_scalar(0, 0)
         exp(0, 0)
+        pos_vector(0, 0)
         for j in range(1, PACK):
             clamp_vector(0, j)
             exp(0, j)
-            combine(0, j - 1)
-        combine(0, PACK - 1)
-        clamp_vector(1, 0)
+            if j > 1:
+                neg_vector(0, j - 2)
+            pos_vector(0, j)
+        neg_vector(0, PACK - 2)
+        neg_scalar(0, PACK - 1)
+        pos_vector(1, 0)
         round_state(0)
-        exp(1, 0)
-        for j in range(1, PACK):
+        for j in range(PACK):
             clamp_scalar(1, j)
             exp(1, j)
         tanh(0)
         round_state(1)
         for h in range(1, H):
             tanh(h)
-        weigh(0)
-        combine(1, 0)
+        combine(0, 0)
+        combine(0, 1)
         quantize_state(0)
-        quantize_q(0)
-        multiply(0)
+        quantize_q(0, 0)
+        multiply(0, 0)
+        quantize_q(0, 1)
+        multiply(0, 1)
         for j in range(1, PACK):
-            combine(1, j)
+            pos_vector(1, j)
+        for j in range(PACK):
+            neg_vector(1, j)
+        combine(1, 0)
         gate(0)
-        weigh(1)
-        gate(1)
         quantize_state(1)
-        quantize_q(1)
-        multiply(1)
+        quantize_q(1, 0)
+        multiply(1, 0)
+        combine(1, 1)
+        gate(1)
+        quantize_q(1, 1)
+        multiply(1, 1)
         for h in range(2, H):
             gate(h)

@@ -19,6 +19,7 @@ ROWS = D // PACK
 HEADS_PER_SET = P // ROWS
 SETS = H // HEADS_PER_SET
 DEAL = N // P
+SPLIT = 3
 
 
 def tile_rows_read_elu1_gate_kernel(tc, q, qa, S, og, out):
@@ -34,9 +35,9 @@ def tile_rows_read_elu1_gate_kernel(tc, q, qa, S, og, out):
         q_raw = [tiles(sb, "q_raw%d_" % s, PACK, [P, N], F32) for s in range(SETS)]
         q_neg = [tiles(sb, "q_neg%d_" % s, PACK, [P, N], F32) for s in range(SETS)]
         q_exp = [tiles(sb, "q_exp%d_" % s, PACK, [P, N], F32) for s in range(SETS)]
-        pos = tiles(sb, "pos", SETS, [P, PACK, N], F32)
-        neg = tiles(sb, "neg", SETS, [P, PACK, N], F32)
-        q_bf = [tiles(sb, "q_bf%d_" % s, 2, [P, 2, P, PACK], BF16) for s in range(SETS)]
+        phi = [tiles(sb, "phi%d_" % s, PACK, [P, N], F32) for s in range(SETS)]
+        fq = tiles(sb, "fq", SETS, [P, PACK, N], BF16)
+        q_bf = tiles(sb, "q_bf", SETS, [P, DEAL, P, PACK], BF16)
         q_codes = [tiles(sb, "q_codes%d_" % s, 2, [P, 2 * P], U32) for s in range(SETS)]
         q_scales = [tiles(sb, "q_scales%d_" % s, 2, [P, 2 * P], U8) for s in range(SETS)]
         s_raw = tiles(sb, "s_raw", SETS, [P, PACK, E], F32)
@@ -72,33 +73,44 @@ def tile_rows_read_elu1_gate_kernel(tc, q, qa, S, og, out):
         def exp(s, j):
             nc.scalar.activation(out=q_exp[s][j][:], in_=q_neg[s][j][:], func=ACT.Exp, scale=-1.0)
 
-        def pos_vector(s, j):
-            nc.vector.tensor_scalar(out=pos[s][:, j, :], in0=q_raw[s][j][:], scalar1=0.0, scalar2=qa4[:, j:j + 1],
-                                    op0=ALU.max, op1=ALU.mult)
+        def combine(s, j):
+            nc.vector.scalar_tensor_tensor(out=phi[s][j][:], in0=q_raw[s][j][:], scalar=0.0,
+                                           in1=q_exp[s][j][:], op0=ALU.max, op1=ALU.add)
 
-        def neg_scalar(s, j):
-            nc.scalar.activation(out=neg[s][:, j, :], in_=q_exp[s][j][:], func=ACT.Copy, scale=qa4[:, j:j + 1])
+        def weigh_scalar(s, j):
+            nc.scalar.activation(out=fq[s][:, j, :], in_=phi[s][j][:], func=ACT.Copy, scale=qa4[:, j:j + 1])
 
-        def neg_vector(s, j):
-            nc.vector.tensor_scalar(out=neg[s][:, j, :], in0=q_exp[s][j][:], scalar1=qa4[:, j:j + 1], scalar2=None,
+        def weigh_vector(s, j):
+            nc.vector.tensor_scalar(out=fq[s][:, j, :], in0=phi[s][j][:], scalar1=qa4[:, j:j + 1], scalar2=None,
                                     op0=ALU.mult)
 
-        def combine(s, a):
-            nc.vector.tensor_tensor(
-                out=q_bf[s][a][:].rearrange("p b m j -> p m j b"),
-                in0=pos[s][:].rearrange("p j (m a b) -> p a m j b", a=2, b=2)[:, a],
-                in1=neg[s][:].rearrange("p j (m a b) -> p a m j b", a=2, b=2)[:, a],
-                op=ALU.add)
+        def interleave_views(s, pairs):
+            return (q_bf[s][:].rearrange("p r (u v) j -> p u r v j", v=2)[:, :, pairs],
+                    fq[s][:].rearrange("p j (u v r) -> p u r v j", v=2, r=DEAL)[:, :, pairs])
+
+        def interleave(s):
+            dst, src = interleave_views(s, slice(0, DEAL))
+            nc.vector.tensor_copy(out=dst, in_=src)
+
+        def interleave_vector(s):
+            dst, src = interleave_views(s, slice(0, SPLIT))
+            nc.vector.tensor_copy(out=dst, in_=src)
+
+        def interleave_scalar(s):
+            dst, src = interleave_views(s, slice(SPLIT, DEAL))
+            nc.scalar.copy(out=dst, in_=src)
 
         def quantize_q(s, a):
             nc.vector.quantize_mx(out=q_codes[s][a][:].bitcast(FP8X4), scales=q_scales[s][a][:],
-                                  in_=q_bf[s][a][:].rearrange("p b m j -> p (b m j)"))
+                                  in_=q_bf[s][:, 2 * a:2 * a + 2].rearrange("p b m j -> p (b m j)"))
 
-        def round_state(s):
-            nc.scalar.activation(
-                out=s_bf[s][:].rearrange("p (c i) j -> p c j i", i=4),
-                in_=s_raw[s][:].rearrange("p j (c i) -> p c j i", i=4),
-                func=ACT.Copy, scale=0.5)
+        def round_state_scalar(s):
+            nc.scalar.activation(out=s_bf[s][:], in_=s_raw[s][:].rearrange("p j e -> p e j"),
+                                 func=ACT.Copy, scale=0.5)
+
+        def round_state_vector(s):
+            nc.vector.tensor_scalar(out=s_bf[s][:], in0=s_raw[s][:].rearrange("p j e -> p e j"),
+                                    scalar1=0.5, scalar2=None, op0=ALU.mult)
 
         def quantize_state(s):
             nc.vector.quantize_mx(out=s_codes[s][:].bitcast(FP8X4), scales=s_scales[s][:],
@@ -124,59 +136,95 @@ def tile_rows_read_elu1_gate_kernel(tc, q, qa, S, og, out):
                                            op0=ALU.add, op1=ALU.mult)
             nc.sync.dma_start(out=out[h].rearrange("(m r) e -> m (r e)", r=DEAL), in_=result[h][:])
 
-        nc.scalar.dma_start(
-            out=qa4[:],
-            in_=qa.rearrange("d o -> (d o)").partition_broadcast(HEADS_PER_SET).rearrange("c (p j) -> c p j", j=PACK))
-        for j in range(PACK):
-            load_q(0, j)
+        def gate_half(h, a):
+            cols = slice(a * 2 * E, (a + 1) * 2 * E)
+            nc.vector.scalar_tensor_tensor(out=result[h][:, cols], in0=og_tanh[h][:, cols], scalar=1.0,
+                                           in1=y[h][:, cols], op0=ALU.add, op1=ALU.mult)
+            nc.sync.dma_start(out=out[h].rearrange("(m r) e -> m (r e)", r=DEAL)[:, cols], in_=result[h][:, cols])
+
+        def load_weights(unused):
+            nc.sync.dma_start(
+                out=qa4[:],
+                in_=qa.rearrange("d o -> (d o)").partition_broadcast(HEADS_PER_SET).rearrange("c (p j) -> c p j", j=PACK))
+
+        load_q(0, 0)
+        load_q(0, 1)
+        load_q(0, 2)
+        load_q(0, 3)
+        load_weights(0)
         load_q(1, 0)
+        load_q(1, 1)
         load_state(0)
-        for j in range(1, PACK):
-            load_q(1, j)
+        load_q(1, 2)
+        load_q(1, 3)
         load_gate(0)
         load_state(1)
-        for h in range(1, H):
-            load_gate(h)
-
-        clamp_scalar(0, 0)
+        load_gate(1)
+        load_gate(2)
+        load_gate(3)
+        load_gate(4)
+        load_gate(5)
+        load_gate(6)
+        load_gate(7)
+        clamp_vector(0, 0)
+        clamp_vector(0, 1)
+        clamp_vector(0, 2)
         exp(0, 0)
-        pos_vector(0, 0)
-        for j in range(1, PACK):
-            clamp_vector(0, j)
-            exp(0, j)
-            if j > 1:
-                neg_vector(0, j - 2)
-            pos_vector(0, j)
-        neg_vector(0, PACK - 2)
-        neg_scalar(0, PACK - 1)
-        pos_vector(1, 0)
-        round_state(0)
-        for j in range(PACK):
-            clamp_scalar(1, j)
-            exp(1, j)
-        tanh(0)
-        round_state(1)
-        for h in range(1, H):
-            tanh(h)
+        exp(0, 1)
+        exp(0, 2)
         combine(0, 0)
+        clamp_vector(0, 3)
         combine(0, 1)
+        combine(0, 2)
+        exp(0, 3)
+        weigh_scalar(0, 0)
+        weigh_scalar(0, 1)
+        weigh_scalar(0, 2)
+        combine(0, 3)
+        clamp_vector(1, 0)
+        clamp_vector(1, 1)
+        clamp_vector(1, 2)
+        clamp_vector(1, 3)
+        weigh_scalar(0, 3)
+        round_state_scalar(0)
+        exp(1, 0)
+        exp(1, 1)
+        exp(1, 2)
+        exp(1, 3)
+        tanh(0)
+        interleave(0)
         quantize_state(0)
         quantize_q(0, 0)
         multiply(0, 0)
         quantize_q(0, 1)
         multiply(0, 1)
-        for j in range(1, PACK):
-            pos_vector(1, j)
-        for j in range(PACK):
-            neg_vector(1, j)
         combine(1, 0)
+        combine(1, 1)
+        combine(1, 2)
+        combine(1, 3)
         gate(0)
+        weigh_vector(1, 3)
+        weigh_scalar(1, 0)
+        weigh_scalar(1, 1)
+        weigh_scalar(1, 2)
+        round_state_scalar(1)
+        tanh(1)
+        tanh(2)
+        tanh(3)
+        tanh(4)
+        tanh(5)
+        tanh(6)
+        tanh(7)
+        interleave(1)
         quantize_state(1)
         quantize_q(1, 0)
         multiply(1, 0)
-        combine(1, 1)
-        gate(1)
         quantize_q(1, 1)
         multiply(1, 1)
-        for h in range(2, H):
-            gate(h)
+        gate(1)
+        gate(2)
+        gate(3)
+        gate(4)
+        gate(5)
+        gate(6)
+        gate(7)

@@ -19,7 +19,8 @@ ROWS = D // PACK
 HEADS_PER_SET = P // ROWS
 SETS = H // HEADS_PER_SET
 DEAL = N // P
-SPLIT = 3
+CHUNK_PLACES = (1, 2)
+FIRST, SECOND = 0, 1
 
 
 def tile_rows_read_elu1_gate_kernel(tc, q, qa, S, og, out):
@@ -29,202 +30,145 @@ def tile_rows_read_elu1_gate_kernel(tc, q, qa, S, og, out):
         ps = ctx.enter_context(tc.psum_pool(name="ps", bufs=1))
         ctx.enter_context(tc.manual_schedule())
 
-        def tiles(pool, name, count, shape, dtype):
-            return [pool.tile(shape, dtype, name="%s%d" % (name, i), align_bytes=64) for i in range(count)]
+        def tiles(name, count, shape, dtype):
+            return [sb.tile(shape, dtype, name="%s%d" % (name, i), align_bytes=64) for i in range(count)]
 
-        q_raw = [tiles(sb, "q_raw%d_" % s, PACK, [P, N], F32) for s in range(SETS)]
-        q_neg = [tiles(sb, "q_neg%d_" % s, PACK, [P, N], F32) for s in range(SETS)]
-        q_exp = [tiles(sb, "q_exp%d_" % s, PACK, [P, N], F32) for s in range(SETS)]
-        phi = [tiles(sb, "phi%d_" % s, PACK, [P, N], F32) for s in range(SETS)]
-        fq = tiles(sb, "fq", SETS, [P, PACK, N], BF16)
-        q_bf = tiles(sb, "q_bf", SETS, [P, DEAL, P, PACK], BF16)
-        q_codes = [tiles(sb, "q_codes%d_" % s, 2, [P, 2 * P], U32) for s in range(SETS)]
-        q_scales = [tiles(sb, "q_scales%d_" % s, 2, [P, 2 * P], U8) for s in range(SETS)]
-        s_raw = tiles(sb, "s_raw", SETS, [P, PACK, E], F32)
-        s_bf = tiles(sb, "s_bf", SETS, [P, E, PACK], BF16)
-        s_codes = tiles(sb, "s_codes", SETS, [P, E], U32)
-        s_scales = tiles(sb, "s_scales", SETS, [P, E], U8)
-        og_raw = tiles(sb, "og_raw", H, [P, DEAL * E], F32)
-        og_tanh = tiles(sb, "og_tanh", H, [P, DEAL * E], F32)
-        result = tiles(sb, "result", H, [P, DEAL * E], F32)
+        def chunk_tiles(name):
+            return [tiles("%s%d_" % (name, s), PACK // CHUNK_PLACES[s], [P, CHUNK_PLACES[s], N], F32)
+                    for s in range(SETS)]
+
+        q_raw = chunk_tiles("q_raw")
+        q_neg = chunk_tiles("q_neg")
+        q_exp = chunk_tiles("q_exp")
+        phi = tiles("phi", SETS, [P, PACK, N], F32)
+        q_bf = tiles("q_bf", SETS, [P, DEAL, P, PACK], BF16)
+        q_codes = tiles("q_codes", SETS, [P, N], U32)
+        q_scales = tiles("q_scales", SETS, [P, N], U8)
+        s_raw = tiles("s_raw", SETS, [P, PACK, E], F32)
+        s_bf = tiles("s_bf", SETS, [P, E, PACK], BF16)
+        s_codes = tiles("s_codes", SETS, [P, E], U32)
+        s_scales = tiles("s_scales", SETS, [P, E], U8)
+        og_raw = tiles("og_raw", H, [P, DEAL * E], F32)
+        og_tanh = tiles("og_tanh", H, [P, DEAL * E], F32)
+        result = tiles("result", H, [P, DEAL * E], F32)
         qa4 = sb.tile([P, PACK], F32, align_bytes=64)
         y = [ps.tile([P, DEAL * E], F32, name="y%d" % h) for h in range(H)]
 
         def heads(s):
             return slice(s * HEADS_PER_SET, (s + 1) * HEADS_PER_SET)
 
-        def load_q(s, j):
+        def places(s, k):
+            return slice(k * CHUNK_PLACES[s], (k + 1) * CHUNK_PLACES[s])
+
+        def chunks(s):
+            return range(PACK // CHUNK_PLACES[s])
+
+        def by_partition(x):
+            return x.rearrange("(m r) e -> m (r e)", r=DEAL)
+
+        def load_q(s):
             rows = q[heads(s)].rearrange("c (p j) n -> (c p) j n", j=PACK)
-            nc.sync.dma_start(out=q_raw[s][j][:], in_=rows[:, j, :])
+            for k in chunks(s):
+                nc.sync.dma_start(out=q_raw[s][k][:], in_=rows[:, places(s, k), :])
+
+        def load_weights():
+            per_head = qa.rearrange("d o -> (d o)").partition_broadcast(HEADS_PER_SET)
+            nc.sync.dma_start(out=qa4[:], in_=per_head.rearrange("c (p j) -> c p j", j=PACK))
 
         def load_state(s):
             nc.sync.dma_start(out=s_raw[s][:], in_=S[heads(s)].rearrange("c (p j) e -> (c p) j e", j=PACK))
 
         def load_gate(h):
-            nc.sync.dma_start(out=og_raw[h][:], in_=og[h].rearrange("(m r) e -> m (r e)", r=DEAL))
+            nc.sync.dma_start(out=og_raw[h][:], in_=by_partition(og[h]))
 
-        def clamp_vector(s, j):
-            nc.vector.tensor_scalar(out=q_neg[s][j][:], in0=q_raw[s][j][:], scalar1=0.0, scalar2=-1.0,
+        def clamp_on_vector(s, k):
+            nc.vector.tensor_scalar(out=q_neg[s][k][:], in0=q_raw[s][k][:], scalar1=0.0, scalar2=-1.0,
                                     op0=ALU.min, op1=ALU.mult)
 
-        def clamp_scalar(s, j):
-            nc.scalar.activation(out=q_neg[s][j][:], in_=q_raw[s][j][:], func=ACT.Relu, scale=-1.0)
+        def clamp_on_scalar(s, k):
+            nc.scalar.activation(out=q_neg[s][k][:], in_=q_raw[s][k][:], func=ACT.Relu, scale=-1.0)
 
-        def exp(s, j):
-            nc.scalar.activation(out=q_exp[s][j][:], in_=q_neg[s][j][:], func=ACT.Exp, scale=-1.0)
+        def exp(s, k):
+            nc.scalar.activation(out=q_exp[s][k][:], in_=q_neg[s][k][:], func=ACT.Exp, scale=-1.0)
 
-        def combine(s, j):
-            nc.vector.scalar_tensor_tensor(out=phi[s][j][:], in0=q_raw[s][j][:], scalar=0.0,
-                                           in1=q_exp[s][j][:], op0=ALU.max, op1=ALU.add)
+        def feature_map(s, k):
+            nc.vector.scalar_tensor_tensor(out=phi[s][:, places(s, k), :], in0=q_raw[s][k][:], scalar=0.0,
+                                           in1=q_exp[s][k][:], op0=ALU.max, op1=ALU.add)
 
-        def weigh_scalar(s, j):
-            nc.scalar.activation(out=fq[s][:, j, :], in_=phi[s][j][:], func=ACT.Copy, scale=qa4[:, j:j + 1])
+        def weigh(s):
+            nc.vector.tensor_tensor(
+                out=q_bf[s][:].rearrange("p r m j -> p m j r"),
+                in0=phi[s][:].rearrange("p j (m r) -> p m j r", r=DEAL),
+                in1=qa4[:].unsqueeze(1).unsqueeze(3).to_broadcast([P, P, PACK, DEAL]),
+                op=ALU.mult)
 
-        def weigh_vector(s, j):
-            nc.vector.tensor_scalar(out=fq[s][:, j, :], in0=phi[s][j][:], scalar1=qa4[:, j:j + 1], scalar2=None,
-                                    op0=ALU.mult)
-
-        def interleave_views(s, pairs):
-            return (q_bf[s][:].rearrange("p r (u v) j -> p u r v j", v=2)[:, :, pairs],
-                    fq[s][:].rearrange("p j (u v r) -> p u r v j", v=2, r=DEAL)[:, :, pairs])
-
-        def interleave(s):
-            dst, src = interleave_views(s, slice(0, DEAL))
-            nc.vector.tensor_copy(out=dst, in_=src)
-
-        def interleave_vector(s):
-            dst, src = interleave_views(s, slice(0, SPLIT))
-            nc.vector.tensor_copy(out=dst, in_=src)
-
-        def interleave_scalar(s):
-            dst, src = interleave_views(s, slice(SPLIT, DEAL))
-            nc.scalar.copy(out=dst, in_=src)
-
-        def quantize_q(s, a):
-            nc.vector.quantize_mx(out=q_codes[s][a][:].bitcast(FP8X4), scales=q_scales[s][a][:],
-                                  in_=q_bf[s][:, 2 * a:2 * a + 2].rearrange("p b m j -> p (b m j)"))
-
-        def round_state_scalar(s):
+        def round_state(s):
             nc.scalar.activation(out=s_bf[s][:], in_=s_raw[s][:].rearrange("p j e -> p e j"),
                                  func=ACT.Copy, scale=0.5)
 
-        def round_state_vector(s):
-            nc.vector.tensor_scalar(out=s_bf[s][:], in0=s_raw[s][:].rearrange("p j e -> p e j"),
-                                    scalar1=0.5, scalar2=None, op0=ALU.mult)
-
-        def quantize_state(s):
+        def quantize_and_multiply(s):
             nc.vector.quantize_mx(out=s_codes[s][:].bitcast(FP8X4), scales=s_scales[s][:],
                                   in_=s_bf[s][:].rearrange("p e j -> p (e j)"))
-
-        def multiply(s, a):
+            nc.vector.quantize_mx(out=q_codes[s][:].bitcast(FP8X4), scales=q_scales[s][:],
+                                  in_=q_bf[s][:].rearrange("p r m j -> p (r m j)"))
             for c in range(HEADS_PER_SET):
                 rows = slice(c * ROWS, (c + 1) * ROWS)
-                for b in range(2):
-                    cols = slice(b * P, (b + 1) * P)
-                    r = 2 * a + b
+                for r in range(DEAL):
+                    cols = slice(r * P, (r + 1) * P)
                     nc.tensor.matmul_mx(
                         out=y[s * HEADS_PER_SET + c][:, r * E:(r + 1) * E],
-                        lhsT=q_codes[s][a][rows, cols].bitcast(FP8X4), lhsT_scale=q_scales[s][a][rows, cols],
+                        lhsT=q_codes[s][rows, cols].bitcast(FP8X4), lhsT_scale=q_scales[s][rows, cols],
                         rhs=s_codes[s][rows, :].bitcast(FP8X4), rhs_scale=s_scales[s][rows, :],
                         start=True, stop=True)
 
         def tanh(h):
             nc.scalar.activation(out=og_tanh[h][:], in_=og_raw[h][:], func=ACT.Tanh, scale=0.5)
 
-        def gate(h):
-            nc.vector.scalar_tensor_tensor(out=result[h][:], in0=og_tanh[h][:], scalar=1.0, in1=y[h][:],
-                                           op0=ALU.add, op1=ALU.mult)
-            nc.sync.dma_start(out=out[h].rearrange("(m r) e -> m (r e)", r=DEAL), in_=result[h][:])
-
-        def gate_half(h, a):
-            cols = slice(a * 2 * E, (a + 1) * 2 * E)
+        def gate_and_store(h, cols):
             nc.vector.scalar_tensor_tensor(out=result[h][:, cols], in0=og_tanh[h][:, cols], scalar=1.0,
                                            in1=y[h][:, cols], op0=ALU.add, op1=ALU.mult)
-            nc.sync.dma_start(out=out[h].rearrange("(m r) e -> m (r e)", r=DEAL)[:, cols], in_=result[h][:, cols])
+            nc.sync.dma_start(out=by_partition(out[h])[:, cols], in_=result[h][:, cols])
 
-        def load_weights(unused):
-            nc.sync.dma_start(
-                out=qa4[:],
-                in_=qa.rearrange("d o -> (d o)").partition_broadcast(HEADS_PER_SET).rearrange("c (p j) -> c p j", j=PACK))
+        whole = slice(0, DEAL * E)
+        halves = (slice(0, DEAL * E // 2), slice(DEAL * E // 2, DEAL * E))
 
-        load_q(0, 0)
-        load_q(0, 1)
-        load_q(0, 2)
-        load_q(0, 3)
-        load_weights(0)
-        load_q(1, 0)
-        load_q(1, 1)
-        load_state(0)
-        load_q(1, 2)
-        load_q(1, 3)
+        load_q(FIRST)
+        load_weights()
+        load_state(FIRST)
+        load_q(SECOND)
         load_gate(0)
-        load_state(1)
-        load_gate(1)
-        load_gate(2)
-        load_gate(3)
-        load_gate(4)
-        load_gate(5)
-        load_gate(6)
-        load_gate(7)
-        clamp_vector(0, 0)
-        clamp_vector(0, 1)
-        clamp_vector(0, 2)
-        exp(0, 0)
-        exp(0, 1)
-        exp(0, 2)
-        combine(0, 0)
-        clamp_vector(0, 3)
-        combine(0, 1)
-        combine(0, 2)
-        exp(0, 3)
-        weigh_scalar(0, 0)
-        weigh_scalar(0, 1)
-        weigh_scalar(0, 2)
-        combine(0, 3)
-        clamp_vector(1, 0)
-        clamp_vector(1, 1)
-        clamp_vector(1, 2)
-        clamp_vector(1, 3)
-        weigh_scalar(0, 3)
-        round_state_scalar(0)
-        exp(1, 0)
-        exp(1, 1)
-        exp(1, 2)
-        exp(1, 3)
+        load_state(SECOND)
+        for h in range(1, H):
+            load_gate(h)
+
+        ahead = 2
+        for k in chunks(FIRST):
+            clamp_on_vector(FIRST, k)
+            exp(FIRST, k)
+            if k >= ahead:
+                feature_map(FIRST, k - ahead)
+        for k in chunks(FIRST)[-ahead:]:
+            feature_map(FIRST, k)
+        round_state(FIRST)
+        weigh(FIRST)
+        quantize_and_multiply(FIRST)
+
+        for k in chunks(SECOND):
+            clamp_on_scalar(SECOND, k)
+        for k in chunks(SECOND):
+            exp(SECOND, k)
+            feature_map(SECOND, k)
+
         tanh(0)
-        interleave(0)
-        quantize_state(0)
-        quantize_q(0, 0)
-        multiply(0, 0)
-        quantize_q(0, 1)
-        multiply(0, 1)
-        combine(1, 0)
-        combine(1, 1)
-        combine(1, 2)
-        combine(1, 3)
-        gate(0)
-        weigh_vector(1, 3)
-        weigh_scalar(1, 0)
-        weigh_scalar(1, 1)
-        weigh_scalar(1, 2)
-        round_state_scalar(1)
+        gate_and_store(0, whole)
+        weigh(SECOND)
         tanh(1)
-        tanh(2)
-        tanh(3)
-        tanh(4)
-        tanh(5)
-        tanh(6)
-        tanh(7)
-        interleave(1)
-        quantize_state(1)
-        quantize_q(1, 0)
-        multiply(1, 0)
-        quantize_q(1, 1)
-        multiply(1, 1)
-        gate(1)
-        gate(2)
-        gate(3)
-        gate(4)
-        gate(5)
-        gate(6)
-        gate(7)
+        gate_and_store(1, whole)
+        round_state(SECOND)
+        quantize_and_multiply(SECOND)
+        for h in range(2, H - 1):
+            tanh(h)
+            gate_and_store(h, whole)
+        tanh(H - 1)
+        for cols in halves:
+            gate_and_store(H - 1, cols)

@@ -95,12 +95,19 @@ def tile_rows_read_elu1_gate_kernel(tc, q, qa, S, og, out):
             nc.vector.scalar_tensor_tensor(out=phi[s][:, places(s, k), :], in0=q_raw[s][k][:], scalar=0.0,
                                            in1=q_exp[s][k][:], op0=ALU.max, op1=ALU.add)
 
-        def weigh(s):
+        def weigh(s, count):
             nc.vector.tensor_tensor(
-                out=q_bf[s][:].rearrange("p r m j -> p m j r"),
-                in0=phi[s][:].rearrange("p j (m r) -> p m j r", r=DEAL),
-                in1=qa4[:].unsqueeze(1).unsqueeze(3).to_broadcast([P, P, PACK, DEAL]),
+                out=q_bf[s][:].rearrange("p r m j -> p m j r")[:, :, :, 0:count],
+                in0=phi[s][:].rearrange("p j (m r) -> p m j r", r=DEAL)[:, :, :, 0:count],
+                in1=qa4[:].unsqueeze(1).unsqueeze(3).to_broadcast([P, P, PACK, count]),
                 op=ALU.mult)
+
+        def weigh_on_scalar(s, r):
+            for j in range(PACK):
+                nc.scalar.activation(
+                    out=q_bf[s][:, r, :, j],
+                    in_=phi[s][:].rearrange("p j (m r) -> p j r m", r=DEAL)[:, j, r, :],
+                    func=ACT.Copy, scale=qa4[:, j:j + 1])
 
         def round_state(s):
             nc.scalar.activation(out=s_bf[s][:], in_=s_raw[s][:].rearrange("p j e -> p e j"),
@@ -150,7 +157,7 @@ def tile_rows_read_elu1_gate_kernel(tc, q, qa, S, og, out):
         for k in chunks(FIRST)[-ahead:]:
             feature_map(FIRST, k)
         round_state(FIRST)
-        weigh(FIRST)
+        weigh(FIRST, DEAL)
         quantize_and_multiply(FIRST)
 
         for k in chunks(SECOND):
@@ -161,10 +168,11 @@ def tile_rows_read_elu1_gate_kernel(tc, q, qa, S, og, out):
 
         tanh(0)
         gate_and_store(0, whole)
-        weigh(SECOND)
+        weigh(SECOND, DEAL - 1)
         tanh(1)
         gate_and_store(1, whole)
         round_state(SECOND)
+        weigh_on_scalar(SECOND, DEAL - 1)
         quantize_and_multiply(SECOND)
         for h in range(2, H - 1):
             tanh(h)

from contextlib import ExitStack

import concourse.mybir as mybir

H, D, N, E = 8, 128, 512, 128
FLOPS = 2 * H * N * D * E

F32 = mybir.dt.float32
BF16 = mybir.dt.bfloat16
U32 = mybir.dt.uint32
U8 = mybir.dt.uint8
FP8X4 = mybir.dt.float8_e4m3fn_x4
ACT = mybir.ActivationFunctionType
ALU = mybir.AluOpType

P = 128
PACK = 4
ROWS = D // PACK
HEADS_PER_SET = P // ROWS
SETS = H // HEADS_PER_SET
DEAL = N // P
CHUNK_PLACES = (1, 2)
FIRST, SECOND = 0, 1


def tile_rows_read_elu1_gate_kernel(tc, q, qa, S, og, out):
    nc = tc.nc
    with ExitStack() as ctx:
        sb = ctx.enter_context(tc.tile_pool(name="sb", bufs=1))
        ps = ctx.enter_context(tc.psum_pool(name="ps", bufs=1))
        ctx.enter_context(tc.manual_schedule())

        def tiles(name, count, shape, dtype):
            return [sb.tile(shape, dtype, name="%s%d" % (name, i), align_bytes=64) for i in range(count)]

        def chunk_tiles(name):
            return [tiles("%s%d_" % (name, s), PACK // CHUNK_PLACES[s], [P, CHUNK_PLACES[s], N], F32)
                    for s in range(SETS)]

        q_raw = chunk_tiles("q_raw")
        q_neg = chunk_tiles("q_neg")
        q_exp = chunk_tiles("q_exp")
        phi = tiles("phi", SETS, [P, PACK, N], F32)
        q_bf = tiles("q_bf", SETS, [P, DEAL, P, PACK], BF16)
        q_codes = tiles("q_codes", SETS, [P, N], U32)
        q_scales = tiles("q_scales", SETS, [P, N], U8)
        s_raw = tiles("s_raw", SETS, [P, PACK, E], F32)
        s_bf = tiles("s_bf", SETS, [P, E, PACK], BF16)
        s_codes = tiles("s_codes", SETS, [P, E], U32)
        s_scales = tiles("s_scales", SETS, [P, E], U8)
        og_raw = tiles("og_raw", H, [P, DEAL * E], F32)
        og_tanh = tiles("og_tanh", H, [P, DEAL * E], F32)
        result = tiles("result", H, [P, DEAL * E], F32)
        qa4 = sb.tile([P, PACK], F32, align_bytes=64)
        y = [ps.tile([P, DEAL * E], F32, name="y%d" % h) for h in range(H)]

        def heads(s):
            return slice(s * HEADS_PER_SET, (s + 1) * HEADS_PER_SET)

        def places(s, k):
            return slice(k * CHUNK_PLACES[s], (k + 1) * CHUNK_PLACES[s])

        def chunks(s):
            return range(PACK // CHUNK_PLACES[s])

        def by_partition(x):
            return x.rearrange("(m r) e -> m (r e)", r=DEAL)

        def load_q(s):
            rows = q[heads(s)].rearrange("c (p j) n -> (c p) j n", j=PACK)
            for k in chunks(s):
                nc.sync.dma_start(out=q_raw[s][k][:], in_=rows[:, places(s, k), :])

        def load_weights():
            per_head = qa.rearrange("d o -> (d o)").partition_broadcast(HEADS_PER_SET)
            nc.sync.dma_start(out=qa4[:], in_=per_head.rearrange("c (p j) -> c p j", j=PACK))

        def load_state(s):
            nc.sync.dma_start(out=s_raw[s][:], in_=S[heads(s)].rearrange("c (p j) e -> (c p) j e", j=PACK))

        def load_gate(h):
            nc.sync.dma_start(out=og_raw[h][:], in_=by_partition(og[h]))

        def clamp_on_vector(s, k):
            nc.vector.tensor_scalar(out=q_neg[s][k][:], in0=q_raw[s][k][:], scalar1=0.0, scalar2=-1.0,
                                    op0=ALU.min, op1=ALU.mult)

        def clamp_on_scalar(s, k):
            nc.scalar.activation(out=q_neg[s][k][:], in_=q_raw[s][k][:], func=ACT.Relu, scale=-1.0)

        def exp(s, k):
            nc.scalar.activation(out=q_exp[s][k][:], in_=q_neg[s][k][:], func=ACT.Exp, scale=-1.0)

        def feature_map(s, k):
            nc.vector.scalar_tensor_tensor(out=phi[s][:, places(s, k), :], in0=q_raw[s][k][:], scalar=0.0,
                                           in1=q_exp[s][k][:], op0=ALU.max, op1=ALU.add)

        def weigh(s, count):
            nc.vector.tensor_tensor(
                out=q_bf[s][:].rearrange("p r m j -> p m j r")[:, :, :, 0:count],
                in0=phi[s][:].rearrange("p j (m r) -> p m j r", r=DEAL)[:, :, :, 0:count],
                in1=qa4[:].unsqueeze(1).unsqueeze(3).to_broadcast([P, P, PACK, count]),
                op=ALU.mult)

        def weigh_on_scalar(s, r):
            for j in range(PACK):
                nc.scalar.activation(
                    out=q_bf[s][:, r, :, j],
                    in_=phi[s][:].rearrange("p j (m r) -> p j r m", r=DEAL)[:, j, r, :],
                    func=ACT.Copy, scale=qa4[:, j:j + 1])

        def round_state(s):
            nc.scalar.activation(out=s_bf[s][:], in_=s_raw[s][:].rearrange("p j e -> p e j"),
                                 func=ACT.Copy, scale=0.5)

        def quantize_and_multiply(s):
            nc.vector.quantize_mx(out=s_codes[s][:].bitcast(FP8X4), scales=s_scales[s][:],
                                  in_=s_bf[s][:].rearrange("p e j -> p (e j)"))
            nc.vector.quantize_mx(out=q_codes[s][:].bitcast(FP8X4), scales=q_scales[s][:],
                                  in_=q_bf[s][:].rearrange("p r m j -> p (r m j)"))
            for c in range(HEADS_PER_SET):
                rows = slice(c * ROWS, (c + 1) * ROWS)
                for r in range(DEAL):
                    cols = slice(r * P, (r + 1) * P)
                    nc.tensor.matmul_mx(
                        out=y[s * HEADS_PER_SET + c][:, r * E:(r + 1) * E],
                        lhsT=q_codes[s][rows, cols].bitcast(FP8X4), lhsT_scale=q_scales[s][rows, cols],
                        rhs=s_codes[s][rows, :].bitcast(FP8X4), rhs_scale=s_scales[s][rows, :],
                        start=True, stop=True)

        def tanh(h):
            nc.scalar.activation(out=og_tanh[h][:], in_=og_raw[h][:], func=ACT.Tanh, scale=0.5)

        def gate_and_store(h, cols):
            nc.vector.scalar_tensor_tensor(out=result[h][:, cols], in0=og_tanh[h][:, cols], scalar=1.0,
                                           in1=y[h][:, cols], op0=ALU.add, op1=ALU.mult)
            nc.sync.dma_start(out=by_partition(out[h])[:, cols], in_=result[h][:, cols])

        whole = slice(0, DEAL * E)
        halves = (slice(0, DEAL * E // 2), slice(DEAL * E // 2, DEAL * E))

        load_q(FIRST)
        load_weights()
        load_state(FIRST)
        load_q(SECOND)
        load_gate(0)
        load_state(SECOND)
        for h in range(1, H):
            load_gate(h)

        ahead = 2
        for k in chunks(FIRST):
            clamp_on_vector(FIRST, k)
            exp(FIRST, k)
            if k >= ahead:
                feature_map(FIRST, k - ahead)
        for k in chunks(FIRST)[-ahead:]:
            feature_map(FIRST, k)
        round_state(FIRST)
        weigh(FIRST, DEAL)
        quantize_and_multiply(FIRST)

        for k in chunks(SECOND):
            clamp_on_scalar(SECOND, k)
        for k in chunks(SECOND):
            exp(SECOND, k)
            feature_map(SECOND, k)

        tanh(0)
        gate_and_store(0, whole)
        weigh(SECOND, DEAL - 1)
        tanh(1)
        gate_and_store(1, whole)
        round_state(SECOND)
        weigh_on_scalar(SECOND, DEAL - 1)
        quantize_and_multiply(SECOND)
        for h in range(2, H - 1):
            tanh(h)
            gate_and_store(h, whole)
        tanh(H - 1)
        for cols in halves:
            gate_and_store(H - 1, cols)
